import numpy as np, ml_dtypes
CORES = [31,71,111]
N = 3
C = 512
def setup_inputs(rng):
    x = 150 * rng.standard_normal((1, 128, C), dtype=np.float32) + 2 * rng.standard_normal((N, 128, C), dtype=np.float32)
    x = (x + rng.uniform(100, 300, (1, 128, C)) * (rng.random((1, 128, C)) < 0.7) * (rng.random((N, 128, C)) < 0.5)).astype(np.float32)
    return {"x": x}
def setup_inputs_trail(rng):
    d = setup_inputs(rng); x = d["x"].copy(); t = int(rng.integers(N))
    x[t] = np.delete(x, t, axis=0).max(axis=0) - rng.uniform(3.0, 20.0, x[t].shape).astype(np.float32)
    return {"x": x}
def reference(x):
    X = x.astype(np.float64)
    P = np.exp(X - X.max(axis=0))
    return {"y": (P / P.sum(axis=0)).astype(ml_dtypes.bfloat16)}

@@ -1,0 +1,148 @@
+from concourse.mybir import AluOpType, ActivationFunctionType
+
+C = 512
+BW = 128
+NB = C // BW
+LATE = [(0, 256), (256, 512)]
+STORES = [(0, 2), (2, 4)]
+CLIP = 87.0
+
+SCRATCH = {
+    "xs": ("sbuf", [128, C], "float32"),
+    "le": ("sbuf", [128, C], "float32"),
+    "ll": ("sbuf", [128, C], "float32"),
+    "de": ("sbuf", [128, C], "float32"),
+    "dl": ("sbuf", [128, C], "float32"),
+    "ee": ("sbuf", [128, C], "bfloat16"),
+    "el": ("sbuf", [128, C], "bfloat16"),
+    "rc": ("sbuf", [128, C], "float32"),
+    "yb": ("sbuf", [128, C], "bfloat16"),
+    "ones": ("sbuf", [128, BW], "bfloat16"),
+    "ident": ("sbuf", [128, 128], "bfloat16"),
+    "xp": ("psum", [128, 512], "float32"),
+}
+for _b in range(NB):
+    SCRATCH["s%d" % _b] = ("psum", [128, 512], "float32")
+
+SEMAPHORES = ["ld", "xpc", "one", "idn", "ae", "sent"]
+SEMAPHORES += ["al%d" % i for i in range(len(LATE))]
+SEMAPHORES += ["st%d" % i for i in range(len(STORES))]
+for _b in range(NB):
+    SEMAPHORES += [n + str(_b) for n in ("de", "te", "ee", "dl", "tl", "el", "sm", "rc", "ct")]
+
+
+def rank_program(g, core, T, topo):
+    rank = T.rank_of(core)
+    if rank is None:
+        return
+    n = len(T.cores)
+    nxt = T.cores[(rank + 1) % n]
+    prv = T.cores[(rank - 1) % n]
+    for dst in (nxt, prv):
+        if not topo.may_write(core, dst):
+            raise ValueError("core %d owns no port towards core %d" % (core, dst))
+    sem = T.sem
+    V, S, PE, SY = g.vector, g.scalar, g.tensor, g.sync
+    Act = ActivationFunctionType
+
+    def blk(b):
+        return slice(b * BW, (b + 1) * BW)
+
+    SY.dma_start(T.xs[:], T.x[:]).then_inc(sem.ld, 16)
+
+    V.memset(T.ones[:], 1.0).then_inc(sem.one, 1)
+    g.wait_ge(sem.one, 1)
+    g.affine_select(T.ident[:], T.ones[:, 0:128], [[-1, 128]], AluOpType.is_equal, 0.0, 0, 1).then_inc(sem.idn, 1)
+    g.wait_ge(sem.ld, 16)
+    sent = 0
+
+    def engines(mask):
+        return sum((mask >> e) & 1 for e in range(16))
+
+    rid, pid, _ = topo.addr(nxt)
+    m_n = topo.mask(core, nxt)
+    g.remote_dma(T.le[:], T.xs[:], sem.ae, sem.sent, pid, rid, m_n)
+    sent += engines(m_n)
+    rid, pid, _ = topo.addr(prv)
+    m_p = topo.mask(core, prv)
+    for i, (a, b) in enumerate(LATE):
+        g.remote_dma(T.ll[:, a:b], T.xs[:, a:b], sem["al%d" % i], sem.sent, pid, rid, m_p)
+        sent += engines(m_p)
+    n_e = engines(topo.mask(prv, core))
+    n_l = engines(topo.mask(nxt, core))
+
+    S.wait_ge(sem.ld, 16)
+    S.activation(T.xp[:, 0:C], T.xs[:], Act.Copy).then_inc(sem.xpc, 1)
+
+    PE.wait_ge(sem.one, 1)
+    for b in range(NB):
+        PE.matmul(T["s%d" % b][:, 0:BW], T.ones[0:1, 0:128], T.ones[0:1, 0:BW], True, False)
+    PE.wait_ge(sem.idn, 1)
+
+    def v_sub(which, b):
+        land, d = (T.le, T.de) if which == "e" else (T.ll, T.dl)
+        V.tensor_tensor(d[:, blk(b)], T.xp[:, blk(b)], land[:, blk(b)], AluOpType.subtract).then_inc(sem["d%s%d" % (which, b)], 1)
+
+    def s_exp(which, b):
+        d, e = (T.de, T.ee) if which == "e" else (T.dl, T.el)
+        S.wait_ge(sem["d%s%d" % (which, b)], 1)
+        S.activation(d[:, blk(b)], d[:, blk(b)], Act.Relu, bias=CLIP, scale=1.0).then_inc(sem["t%s%d" % (which, b)], 1)
+        S.wait_ge(sem["t%s%d" % (which, b)], 1)
+        S.activation(e[:, blk(b)], d[:, blk(b)], Act.Exp, bias=CLIP, scale=-1.0).then_inc(sem["e%s%d" % (which, b)], 1)
+
+    def pe_add(which, b, last):
+        e = T.ee if which == "e" else T.el
+        PE.wait_ge(sem["e%s%d" % (which, b)], 1)
+        mm = PE.matmul(T["s%d" % b][:, 0:BW], T.ident[:], e[:, blk(b)], False, last)
+        if last:
+            mm.then_inc(sem["sm%d" % b], 1)
+
+    def v_recip(b):
+        V.wait_ge(sem["sm%d" % b], 1)
+        V.reciprocal(T.rc[:, blk(b)], T["s%d" % b][:, 0:BW]).then_inc(sem["rc%d" % b], 1)
+
+    def s_cast(b):
+        S.wait_ge(sem["rc%d" % b], 1)
+        S.activation(T.yb[:, blk(b)], T.rc[:, blk(b)], Act.Copy).then_inc(sem["ct%d" % b], 1)
+
+    V.wait_ge(sem.xpc, 1)
+    V.wait_ge(sem.ae, n_e)
+    for b in range(NB):
+        v_sub("e", b)
+    for i, (a, z) in enumerate(LATE):
+        V.wait_ge(sem["al%d" % i], n_l)
+        bs = range(a // BW, z // BW)
+        for b in bs:
+            v_sub("l", b)
+        for b in bs:
+            v_recip(b)
+
+    first = list(range(LATE[0][0] // BW, LATE[0][1] // BW))
+    rest = [b for b in range(NB) if b not in first]
+    for b in first:
+        s_exp("e", b)
+        s_exp("l", b)
+    for b in rest:
+        s_exp("e", b)
+    for b in first:
+        s_cast(b)
+    for b in rest:
+        s_exp("l", b)
+    for b in rest:
+        s_cast(b)
+
+    for b in first:
+        pe_add("e", b, False)
+        pe_add("l", b, True)
+    for b in rest:
+        pe_add("e", b, False)
+    for b in rest:
+        pe_add("l", b, True)
+
+    for i, (b0, b1) in enumerate(STORES):
+        for b in range(b0, b1):
+            SY.wait_ge(sem["ct%d" % b], 1)
+        SY.dma_start(T.y[:, b0 * BW:b1 * BW], T.yb[:, b0 * BW:b1 * BW]).then_inc(sem["st%d" % i], 16)
+    for i in range(len(STORES)):
+        SY.wait_ge(sem["st%d" % i], 16)
+    g.wait_ge(sem.sent, sent)

@@ -3,7 +3,7 @@ from concourse.mybir import AluOpType, ActivationFunctionType
 C = 512
 BW = 128
 NB = C // BW
-LATE = [(0, 256), (256, 512)]
+HALF = [(0, 256), (256, 512)]
 STORES = [(0, 2), (2, 4)]
 CLIP = 87.0
 
@@ -24,8 +24,9 @@ SCRATCH = {
 for _b in range(NB):
     SCRATCH["s%d" % _b] = ("psum", [128, 512], "float32")
 
-SEMAPHORES = ["ld", "xpc", "one", "idn", "ae", "sent"]
-SEMAPHORES += ["al%d" % i for i in range(len(LATE))]
+SEMAPHORES = ["one", "idn", "sent"]
+for _i in range(len(HALF)):
+    SEMAPHORES += [n + str(_i) for n in ("ld", "xpc", "ae", "al")]
 SEMAPHORES += ["st%d" % i for i in range(len(STORES))]
 for _b in range(NB):
     SEMAPHORES += [n + str(_b) for n in ("de", "te", "ee", "dl", "tl", "el", "sm", "rc", "ct")]
@@ -48,31 +49,30 @@ def rank_program(g, core, T, topo):
     def blk(b):
         return slice(b * BW, (b + 1) * BW)
 
-    SY.dma_start(T.xs[:], T.x[:]).then_inc(sem.ld, 16)
+    for i, (a, z) in enumerate(HALF):
+        SY.dma_start(T.xs[:, a:z], T.x[:, a:z]).then_inc(sem["ld%d" % i], 16)
 
     V.memset(T.ones[:], 1.0).then_inc(sem.one, 1)
     g.wait_ge(sem.one, 1)
     g.affine_select(T.ident[:], T.ones[:, 0:128], [[-1, 128]], AluOpType.is_equal, 0.0, 0, 1).then_inc(sem.idn, 1)
-    g.wait_ge(sem.ld, 16)
     sent = 0
 
     def engines(mask):
         return sum((mask >> e) & 1 for e in range(16))
 
-    rid, pid, _ = topo.addr(nxt)
-    m_n = topo.mask(core, nxt)
-    g.remote_dma(T.le[:], T.xs[:], sem.ae, sem.sent, pid, rid, m_n)
-    sent += engines(m_n)
-    rid, pid, _ = topo.addr(prv)
-    m_p = topo.mask(core, prv)
-    for i, (a, b) in enumerate(LATE):
-        g.remote_dma(T.ll[:, a:b], T.xs[:, a:b], sem["al%d" % i], sem.sent, pid, rid, m_p)
-        sent += engines(m_p)
+    for i, (a, z) in enumerate(HALF):
+        g.wait_ge(sem["ld%d" % i], 16)
+        for dst, land, name in ((nxt, T.le, "ae%d"), (prv, T.ll, "al%d")):
+            rid, pid, _ = topo.addr(dst)
+            m = topo.mask(core, dst)
+            g.remote_dma(land[:, a:z], T.xs[:, a:z], sem[name % i], sem.sent, pid, rid, m)
+            sent += engines(m)
     n_e = engines(topo.mask(prv, core))
     n_l = engines(topo.mask(nxt, core))
 
-    S.wait_ge(sem.ld, 16)
-    S.activation(T.xp[:, 0:C], T.xs[:], Act.Copy).then_inc(sem.xpc, 1)
+    for i, (a, z) in enumerate(HALF):
+        S.wait_ge(sem["ld%d" % i], 16)
+        S.activation(T.xp[:, a:z], T.xs[:, a:z], Act.Copy).then_inc(sem["xpc%d" % i], 1)
 
     PE.wait_ge(sem.one, 1)
     for b in range(NB):
@@ -105,26 +105,35 @@ def rank_program(g, core, T, topo):
         S.wait_ge(sem["rc%d" % b], 1)
         S.activation(T.yb[:, blk(b)], T.rc[:, blk(b)], Act.Copy).then_inc(sem["ct%d" % b], 1)
 
-    V.wait_ge(sem.xpc, 1)
-    V.wait_ge(sem.ae, n_e)
-    for b in range(NB):
+    first = list(range(HALF[0][0] // BW, HALF[0][1] // BW))
+    rest = list(range(HALF[1][0] // BW, HALF[1][1] // BW))
+    for i in range(len(HALF)):
+        V.wait_ge(sem["xpc%d" % i], 1)
+    V.wait_ge(sem.ae0, n_e)
+    for b in first:
         v_sub("e", b)
-    for i, (a, z) in enumerate(LATE):
-        V.wait_ge(sem["al%d" % i], n_l)
-        bs = range(a // BW, z // BW)
-        for b in bs:
-            v_sub("l", b)
-        for b in bs:
-            v_recip(b)
+    V.wait_ge(sem.al0, n_l)
+    for b in first:
+        v_sub("l", b)
+    v_recip(first[0])
+    V.wait_ge(sem.ae1, n_e)
+    for b in rest:
+        v_sub("e", b)
+    for b in first[1:]:
+        v_recip(b)
+    V.wait_ge(sem.al1, n_l)
+    for b in rest:
+        v_sub("l", b)
+    for b in rest:
+        v_recip(b)
 
-    first = list(range(LATE[0][0] // BW, LATE[0][1] // BW))
-    rest = [b for b in range(NB) if b not in first]
     for b in first:
         s_exp("e", b)
         s_exp("l", b)
+    s_cast(first[0])
     for b in rest:
         s_exp("e", b)
-    for b in first:
+    for b in first[1:]:
         s_cast(b)
     for b in rest:
         s_exp("l", b)

@@ -4,32 +4,30 @@ C = 512
 BW = 128
 NB = C // BW
 HALF = [(0, 256), (256, 512)]
-STORES = [(0, 2), (2, 4)]
-CLIP = 87.0
+S_, B0, P_, Q_, C0 = 0.9856620329846286, -0.5526687774740315, 0.8233585316291777, 0.9998044627794158, -0.9989902994791405
 
 SCRATCH = {
     "xs": ("sbuf", [128, C], "float32"),
     "le": ("sbuf", [128, C], "float32"),
     "ll": ("sbuf", [128, C], "float32"),
-    "de": ("sbuf", [128, C], "float32"),
-    "dl": ("sbuf", [128, C], "float32"),
-    "ee": ("sbuf", [128, C], "bfloat16"),
-    "el": ("sbuf", [128, C], "bfloat16"),
-    "rc": ("sbuf", [128, C], "float32"),
+    "d": ("sbuf", [128, C], "float32"),
+    "ad": ("sbuf", [128, C], "float32"),
+    "w": ("sbuf", [128, C], "float32"),
+    "q": ("sbuf", [128, C], "float32"),
+    "t": ("sbuf", [128, C], "float32"),
+    "sg": ("sbuf", [128, C], "float32"),
     "yb": ("sbuf", [128, C], "bfloat16"),
-    "ones": ("sbuf", [128, BW], "bfloat16"),
-    "ident": ("sbuf", [128, 128], "bfloat16"),
     "xp": ("psum", [128, 512], "float32"),
+    "mx": ("psum", [128, 512], "float32"),
+    "u0": ("psum", [128, 512], "float32"),
+    "u1": ("psum", [128, 512], "float32"),
 }
-for _b in range(NB):
-    SCRATCH["s%d" % _b] = ("psum", [128, 512], "float32")
 
-SEMAPHORES = ["one", "idn", "sent"]
+SEMAPHORES = ["sent"]
 for _i in range(len(HALF)):
-    SEMAPHORES += [n + str(_i) for n in ("ld", "xpc", "ae", "al")]
-SEMAPHORES += ["st%d" % i for i in range(len(STORES))]
+    SEMAPHORES += [n + str(_i) for n in ("ld", "xpc", "ae", "al", "st")]
 for _b in range(NB):
-    SEMAPHORES += [n + str(_b) for n in ("de", "te", "ee", "dl", "tl", "el", "sm", "rc", "ct")]
+    SEMAPHORES += [n + str(_b) for n in ("d", "m", "ab", "w", "q", "u", "A", "t", "s", "y")]
 
 
 def rank_program(g, core, T, topo):
@@ -43,28 +41,33 @@ def rank_program(g, core, T, topo):
         if not topo.may_write(core, dst):
             raise ValueError("core %d owns no port towards core %d" % (core, dst))
     sem = T.sem
-    V, S, PE, SY = g.vector, g.scalar, g.tensor, g.sync
+    V, S, SY = g.vector, g.scalar, g.sync
     Act = ActivationFunctionType
+    Alu = AluOpType
 
     def blk(b):
         return slice(b * BW, (b + 1) * BW)
 
-    for i, (a, z) in enumerate(HALF):
-        SY.dma_start(T.xs[:, a:z], T.x[:, a:z]).then_inc(sem["ld%d" % i], 16)
+    def blocks(i):
+        return list(range(HALF[i][0] // BW, HALF[i][1] // BW))
 
-    V.memset(T.ones[:], 1.0).then_inc(sem.one, 1)
-    g.wait_ge(sem.one, 1)
-    g.affine_select(T.ident[:], T.ones[:, 0:128], [[-1, 128]], AluOpType.is_equal, 0.0, 0, 1).then_inc(sem.idn, 1)
-    sent = 0
+    def ubuf(b):
+        i = [k for k in range(len(HALF)) if b in blocks(k)][0]
+        return T["u%d" % i][:, blk(b)]
 
     def engines(mask):
         return sum((mask >> e) & 1 for e in range(16))
 
     for i, (a, z) in enumerate(HALF):
-        g.wait_ge(sem["ld%d" % i], 16)
-        for dst, land, name in ((nxt, T.le, "ae%d"), (prv, T.ll, "al%d")):
-            rid, pid, _ = topo.addr(dst)
-            m = topo.mask(core, dst)
+        SY.dma_start(T.xs[:, a:z], T.x[:, a:z]).then_inc(sem["ld%d" % i], 16)
+
+    sent = 0
+    for dst, land, name in ((nxt, T.le, "ae%d"), (prv, T.ll, "al%d")):
+        rid, pid, _ = topo.addr(dst)
+        m = topo.mask(core, dst)
+        for i, (a, z) in enumerate(HALF):
+            if dst == nxt:
+                g.wait_ge(sem["ld%d" % i], 16)
             g.remote_dma(land[:, a:z], T.xs[:, a:z], sem[name % i], sem.sent, pid, rid, m)
             sent += engines(m)
     n_e = engines(topo.mask(prv, core))
@@ -73,85 +76,52 @@ def rank_program(g, core, T, topo):
     for i, (a, z) in enumerate(HALF):
         S.wait_ge(sem["ld%d" % i], 16)
         S.activation(T.xp[:, a:z], T.xs[:, a:z], Act.Copy).then_inc(sem["xpc%d" % i], 1)
-
-    PE.wait_ge(sem.one, 1)
+    for i in range(len(HALF)):
+        bs = blocks(i)
+        for b in bs:
+            S.wait_ge(sem["d%d" % b], 1)
+            S.activation(T.ad[:, blk(b)], T.d[:, blk(b)], Act.Abs).then_inc(sem["ab%d" % b], 1)
+        for b in bs:
+            S.wait_ge(sem["ab%d" % b], 1)
+            S.activation(T.w[:, blk(b)], T.ad[:, blk(b)], Act.Sigmoid, bias=B0, scale=-S_).then_inc(sem["w%d" % b], 1)
+        for b in bs:
+            S.wait_ge(sem["w%d" % b], 1)
+            S.activation(T.q[:, blk(b)], T.w[:, blk(b)], Act.Square, bias=Q_, scale=P_).then_inc(sem["q%d" % b], 1)
+        for b in bs:
+            S.activation(ubuf(b), T.d[:, blk(b)], Act.Sigmoid).then_inc(sem["u%d" % b], 1)
     for b in range(NB):
-        PE.matmul(T["s%d" % b][:, 0:BW], T.ones[0:1, 0:128], T.ones[0:1, 0:BW], True, False)
-    PE.wait_ge(sem.idn, 1)
+        S.wait_ge(sem["t%d" % b], 1)
+        S.activation(T.sg[:, blk(b)], T.t[:, blk(b)], Act.Sigmoid, bias=C0, scale=1.0).then_inc(sem["s%d" % b], 1)
 
-    def v_sub(which, b):
-        land, d = (T.le, T.de) if which == "e" else (T.ll, T.dl)
-        V.tensor_tensor(d[:, blk(b)], T.xp[:, blk(b)], land[:, blk(b)], AluOpType.subtract).then_inc(sem["d%s%d" % (which, b)], 1)
-
-    def s_exp(which, b):
-        d, e = (T.de, T.ee) if which == "e" else (T.dl, T.el)
-        S.wait_ge(sem["d%s%d" % (which, b)], 1)
-        S.activation(d[:, blk(b)], d[:, blk(b)], Act.Relu, bias=CLIP, scale=1.0).then_inc(sem["t%s%d" % (which, b)], 1)
-        S.wait_ge(sem["t%s%d" % (which, b)], 1)
-        S.activation(e[:, blk(b)], d[:, blk(b)], Act.Exp, bias=CLIP, scale=-1.0).then_inc(sem["e%s%d" % (which, b)], 1)
-
-    def pe_add(which, b, last):
-        e = T.ee if which == "e" else T.el
-        PE.wait_ge(sem["e%s%d" % (which, b)], 1)
-        mm = PE.matmul(T["s%d" % b][:, 0:BW], T.ident[:], e[:, blk(b)], False, last)
-        if last:
-            mm.then_inc(sem["sm%d" % b], 1)
-
-    def v_recip(b):
-        V.wait_ge(sem["sm%d" % b], 1)
-        V.reciprocal(T.rc[:, blk(b)], T["s%d" % b][:, 0:BW]).then_inc(sem["rc%d" % b], 1)
-
-    def s_cast(b):
-        S.wait_ge(sem["rc%d" % b], 1)
-        S.activation(T.yb[:, blk(b)], T.rc[:, blk(b)], Act.Copy).then_inc(sem["ct%d" % b], 1)
-
-    first = list(range(HALF[0][0] // BW, HALF[0][1] // BW))
-    rest = list(range(HALF[1][0] // BW, HALF[1][1] // BW))
     for i in range(len(HALF)):
         V.wait_ge(sem["xpc%d" % i], 1)
-    V.wait_ge(sem.ae0, n_e)
-    for b in first:
-        v_sub("e", b)
-    V.wait_ge(sem.al0, n_l)
-    for b in first:
-        v_sub("l", b)
-    v_recip(first[0])
-    V.wait_ge(sem.ae1, n_e)
-    for b in rest:
-        v_sub("e", b)
-    for b in first[1:]:
-        v_recip(b)
-    V.wait_ge(sem.al1, n_l)
-    for b in rest:
-        v_sub("l", b)
-    for b in rest:
-        v_recip(b)
+    for i in range(len(HALF)):
+        bs = blocks(i)
+        V.wait_ge(sem["ae%d" % i], n_e)
+        for b in bs:
+            V.tensor_tensor(T.d[:, blk(b)], T.xp[:, blk(b)], T.le[:, blk(b)], Alu.subtract).then_inc(sem["d%d" % b], 1)
+        for b in bs:
+            V.tensor_tensor(T.mx[:, blk(b)], T.xp[:, blk(b)], T.le[:, blk(b)], Alu.max).then_inc(sem["m%d" % b], 1)
+        for b in bs:
+            V.wait_ge(sem["m%d" % b], 1)
+            V.wait_ge(sem["q%d" % b], 1)
+            V.tensor_tensor(T.mx[:, blk(b)], T.mx[:, blk(b)], T.q[:, blk(b)], Alu.add).then_inc(sem["A%d" % b], 1)
+    for i in range(len(HALF)):
+        bs = blocks(i)
+        V.wait_ge(sem["al%d" % i], n_l)
+        for b in bs:
+            V.wait_ge(sem["A%d" % b], 1)
+            V.tensor_tensor(T.t[:, blk(b)], T.mx[:, blk(b)], T.ll[:, blk(b)], Alu.subtract).then_inc(sem["t%d" % b], 1)
+        for b in bs:
+            V.wait_ge(sem["u%d" % b], 1)
+        for b in bs:
+            V.wait_ge(sem["s%d" % b], 1)
+            V.tensor_tensor(T.yb[:, blk(b)], ubuf(b), T.sg[:, blk(b)], Alu.mult).then_inc(sem["y%d" % b], 1)
 
-    for b in first:
-        s_exp("e", b)
-        s_exp("l", b)
-    s_cast(first[0])
-    for b in rest:
-        s_exp("e", b)
-    for b in first[1:]:
-        s_cast(b)
-    for b in rest:
-        s_exp("l", b)
-    for b in rest:
-        s_cast(b)
-
-    for b in first:
-        pe_add("e", b, False)
-        pe_add("l", b, True)
-    for b in rest:
-        pe_add("e", b, False)
-    for b in rest:
-        pe_add("l", b, True)
-
-    for i, (b0, b1) in enumerate(STORES):
-        for b in range(b0, b1):
-            SY.wait_ge(sem["ct%d" % b], 1)
-        SY.dma_start(T.y[:, b0 * BW:b1 * BW], T.yb[:, b0 * BW:b1 * BW]).then_inc(sem["st%d" % i], 16)
-    for i in range(len(STORES)):
+    for i, (a, z) in enumerate(HALF):
+        for b in blocks(i):
+            SY.wait_ge(sem["y%d" % b], 1)
+        SY.dma_start(T.y[:, a:z], T.yb[:, a:z]).then_inc(sem["st%d" % i], 16)
+    for i in range(len(HALF)):
         SY.wait_ge(sem["st%d" % i], 16)
     g.wait_ge(sem.sent, sent)

@@ -1,9 +1,10 @@
 from concourse.mybir import AluOpType, ActivationFunctionType
 
 C = 512
-BW = 128
-NB = C // BW
-HALF = [(0, 256), (256, 512)]
+W = 96
+W0 = 32
+G0 = 3 * W
+GB = [(G0, G0 + 112), (G0 + 112, C)]
 S_, B0, P_, Q_, C0 = 0.9856620329846286, -0.5526687774740315, 0.8233585316291777, 0.9998044627794158, -0.9989902994791405
 
 SCRATCH = {
@@ -17,17 +18,24 @@ SCRATCH = {
     "t": ("sbuf", [128, C], "float32"),
     "sg": ("sbuf", [128, C], "float32"),
     "yb": ("sbuf", [128, C], "bfloat16"),
+    "yn": ("sbuf", [128, W], "bfloat16"),
+    "yp": ("sbuf", [128, W], "bfloat16"),
     "xp": ("psum", [128, 512], "float32"),
     "mx": ("psum", [128, 512], "float32"),
-    "u0": ("psum", [128, 512], "float32"),
-    "u1": ("psum", [128, 512], "float32"),
+    "uo": ("psum", [128, 512], "float32"),
+    "ug": ("psum", [128, 512], "float32"),
 }
 
-SEMAPHORES = ["sent"]
-for _i in range(len(HALF)):
-    SEMAPHORES += [n + str(_i) for n in ("ld", "xpc", "ae", "al", "st")]
-for _b in range(NB):
-    SEMAPHORES += [n + str(_b) for n in ("d", "m", "ab", "w", "q", "u", "A", "t", "s", "y")]
+SEMAPHORES = ["sent", "aeT", "aeR", "alO", "aeG", "alG", "yfp", "yfn", "xpc", "uO", "tO", "yc", "sO", "ybk", "ya"]
+SEMAPHORES += ["ld%d" % _i for _i in range(5)] + ["st%d" % _i for _i in range(5)]
+for _k in ("O0", "O1", "G0", "G1"):
+    SEMAPHORES += [n + _k for n in ("d", "m", "ab", "w", "q", "A")]
+for _k in ("G0", "G1"):
+    SEMAPHORES += [n + _k for n in ("u", "t", "s", "y")]
+
+
+def engines(mask):
+    return bin(mask).count("1")
 
 
 def rank_program(g, core, T, topo):
@@ -35,8 +43,8 @@ def rank_program(g, core, T, topo):
     if rank is None:
         return
     n = len(T.cores)
-    nxt = T.cores[(rank + 1) % n]
-    prv = T.cores[(rank - 1) % n]
+    rn, rp = (rank + 1) % n, (rank - 1) % n
+    nxt, prv = T.cores[rn], T.cores[rp]
     for dst in (nxt, prv):
         if not topo.may_write(core, dst):
             raise ValueError("core %d owns no port towards core %d" % (core, dst))
@@ -45,83 +53,131 @@ def rank_program(g, core, T, topo):
     Act = ActivationFunctionType
     Alu = AluOpType
 
-    def blk(b):
-        return slice(b * BW, (b + 1) * BW)
+    def sl(p):
+        return slice(p[0], p[1])
 
-    def blocks(i):
-        return list(range(HALF[i][0] // BW, HALF[i][1] // BW))
+    def owned(r):
+        return (W * r, W * r + W)
 
-    def ubuf(b):
-        i = [k for k in range(len(HALF)) if b in blocks(k)][0]
-        return T["u%d" % i][:, blk(b)]
+    own = owned(rank)
+    BL = {"O0": (own[0], own[0] + W0), "O1": (own[0] + W0, own[1]), "G0": GB[0], "G1": GB[1]}
+    O, G = sl(own), slice(G0, C)
+    on, op = owned(rn), owned(rp)
+    first, rest = (on[0], on[0] + W0), (on[0] + W0, on[1])
 
-    def engines(mask):
-        return sum((mask >> e) & 1 for e in range(16))
+    for i, p in enumerate((first, rest, op, own, (G0, C))):
+        SY.dma_start(T.xs[:, sl(p)], T.x[:, sl(p)]).then_inc(sem["ld%d" % i], 16)
 
-    for i, (a, z) in enumerate(HALF):
-        SY.dma_start(T.xs[:, a:z], T.x[:, a:z]).then_inc(sem["ld%d" % i], 16)
+    rid_n, pid_n, _ = topo.addr(nxt)
+    rid_p, pid_p, _ = topo.addr(prv)
+    m_n, m_p = topo.mask(core, nxt), topo.mask(core, prv)
+    g.wait_ge(sem.ld0, 16)
+    g.remote_dma(T.le[:, sl(first)], T.xs[:, sl(first)], sem.aeT, sem.sent, pid_n, rid_n, m_n)
+    g.wait_ge(sem.ld1, 16)
+    g.remote_dma(T.le[:, sl(rest)], T.xs[:, sl(rest)], sem.aeR, sem.sent, pid_n, rid_n, m_n)
+    g.wait_ge(sem.ld2, 16)
+    g.remote_dma(T.ll[:, sl(op)], T.xs[:, sl(op)], sem.alO, sem.sent, pid_p, rid_p, m_p)
+    g.wait_ge(sem.ld4, 16)
+    g.remote_dma(T.le[:, G], T.xs[:, G], sem.aeG, sem.sent, pid_n, rid_n, m_n)
+    g.remote_dma(T.ll[:, G], T.xs[:, G], sem.alG, sem.sent, pid_p, rid_p, m_p)
+    g.wait_ge(sem.yc, 1)
+    g.remote_dma(T.yb[:, O], T.yn[:, :], sem.yfp, sem.sent, pid_n, rid_n, m_n)
+    g.wait_ge(sem.ybk, 1)
+    g.remote_dma(T.yb[:, O], T.yp[:, :], sem.yfn, sem.sent, pid_p, rid_p, m_p)
+    sent = 4 * engines(m_n) + 3 * engines(m_p)
+    n_p = engines(topo.mask(prv, core))
+    n_n = engines(topo.mask(nxt, core))
 
-    sent = 0
-    for dst, land, name in ((nxt, T.le, "ae%d"), (prv, T.ll, "al%d")):
-        rid, pid, _ = topo.addr(dst)
-        m = topo.mask(core, dst)
-        for i, (a, z) in enumerate(HALF):
-            if dst == nxt:
-                g.wait_ge(sem["ld%d" % i], 16)
-            g.remote_dma(land[:, a:z], T.xs[:, a:z], sem[name % i], sem.sent, pid, rid, m)
-            sent += engines(m)
-    n_e = engines(topo.mask(prv, core))
-    n_l = engines(topo.mask(nxt, core))
+    def s_lse(k):
+        b = sl(BL[k])
+        S.wait_ge(sem["d" + k], 1)
+        S.activation(T.ad[:, b], T.d[:, b], Act.Abs).then_inc(sem["ab" + k], 1)
+        S.wait_ge(sem["ab" + k], 1)
+        S.activation(T.w[:, b], T.ad[:, b], Act.Sigmoid, bias=B0, scale=-S_).then_inc(sem["w" + k], 1)
+        S.wait_ge(sem["w" + k], 1)
+        S.activation(T.q[:, b], T.w[:, b], Act.Square, bias=Q_, scale=P_).then_inc(sem["q" + k], 1)
 
-    for i, (a, z) in enumerate(HALF):
-        S.wait_ge(sem["ld%d" % i], 16)
-        S.activation(T.xp[:, a:z], T.xs[:, a:z], Act.Copy).then_inc(sem["xpc%d" % i], 1)
-    for i in range(len(HALF)):
-        bs = blocks(i)
-        for b in bs:
-            S.wait_ge(sem["d%d" % b], 1)
-            S.activation(T.ad[:, blk(b)], T.d[:, blk(b)], Act.Abs).then_inc(sem["ab%d" % b], 1)
-        for b in bs:
-            S.wait_ge(sem["ab%d" % b], 1)
-            S.activation(T.w[:, blk(b)], T.ad[:, blk(b)], Act.Sigmoid, bias=B0, scale=-S_).then_inc(sem["w%d" % b], 1)
-        for b in bs:
-            S.wait_ge(sem["w%d" % b], 1)
-            S.activation(T.q[:, blk(b)], T.w[:, blk(b)], Act.Square, bias=Q_, scale=P_).then_inc(sem["q%d" % b], 1)
-        for b in bs:
-            S.activation(ubuf(b), T.d[:, blk(b)], Act.Sigmoid).then_inc(sem["u%d" % b], 1)
-    for b in range(NB):
-        S.wait_ge(sem["t%d" % b], 1)
-        S.activation(T.sg[:, blk(b)], T.t[:, blk(b)], Act.Sigmoid, bias=C0, scale=1.0).then_inc(sem["s%d" % b], 1)
+    S.wait_ge(sem.ld3, 16)
+    S.activation(T.xp[:, O], T.xs[:, O], Act.Copy).then_inc(sem.xpc, 1)
+    S.wait_ge(sem.ld4, 16)
+    S.activation(T.xp[:, G], T.xs[:, G], Act.Copy).then_inc(sem.xpc, 1)
+    s_lse("O0")
+    s_lse("O1")
+    S.activation(T.uo[:, 0:W], T.d[:, O], Act.Sigmoid).then_inc(sem.uO, 1)
+    S.activation(T.uo[:, 128:128 + W], T.d[:, O], Act.Sigmoid, bias=0.0, scale=-1.0).then_inc(sem.uO, 1)
+    S.wait_ge(sem.tO, 1)
+    S.activation(T.yn[:, :], T.t[:, O], Act.Sigmoid, bias=-C0, scale=-1.0).then_inc(sem.yc, 1)
+    S.activation(T.sg[:, O], T.t[:, O], Act.Sigmoid, bias=C0, scale=1.0).then_inc(sem.sO, 1)
+    for k in ("G0", "G1"):
+        s_lse(k)
+    for k in ("G0", "G1"):
+        b = sl(BL[k])
+        S.activation(T.ug[:, b], T.d[:, b], Act.Sigmoid).then_inc(sem["u" + k], 1)
+    for k in ("G0", "G1"):
+        b = sl(BL[k])
+        S.wait_ge(sem["t" + k], 1)
+        S.activation(T.sg[:, b], T.t[:, b], Act.Sigmoid, bias=C0, scale=1.0).then_inc(sem["s" + k], 1)
+    for i, k in ((3, "G0"), (4, "G1")):
+        b = sl(BL[k])
+        S.wait_ge(sem["y" + k], 1)
+        S.dma_start(T.y[:, b], T.yb[:, b]).then_inc(sem["st%d" % i], 16)
 
-    for i in range(len(HALF)):
-        V.wait_ge(sem["xpc%d" % i], 1)
-    for i in range(len(HALF)):
-        bs = blocks(i)
-        V.wait_ge(sem["ae%d" % i], n_e)
-        for b in bs:
-            V.tensor_tensor(T.d[:, blk(b)], T.xp[:, blk(b)], T.le[:, blk(b)], Alu.subtract).then_inc(sem["d%d" % b], 1)
-        for b in bs:
-            V.tensor_tensor(T.mx[:, blk(b)], T.xp[:, blk(b)], T.le[:, blk(b)], Alu.max).then_inc(sem["m%d" % b], 1)
-        for b in bs:
-            V.wait_ge(sem["m%d" % b], 1)
-            V.wait_ge(sem["q%d" % b], 1)
-            V.tensor_tensor(T.mx[:, blk(b)], T.mx[:, blk(b)], T.q[:, blk(b)], Alu.add).then_inc(sem["A%d" % b], 1)
-    for i in range(len(HALF)):
-        bs = blocks(i)
-        V.wait_ge(sem["al%d" % i], n_l)
-        for b in bs:
-            V.wait_ge(sem["A%d" % b], 1)
-            V.tensor_tensor(T.t[:, blk(b)], T.mx[:, blk(b)], T.ll[:, blk(b)], Alu.subtract).then_inc(sem["t%d" % b], 1)
-        for b in bs:
-            V.wait_ge(sem["u%d" % b], 1)
-        for b in bs:
-            V.wait_ge(sem["s%d" % b], 1)
-            V.tensor_tensor(T.yb[:, blk(b)], ubuf(b), T.sg[:, blk(b)], Alu.mult).then_inc(sem["y%d" % b], 1)
+    def v_d(k):
+        b = sl(BL[k])
+        V.tensor_tensor(T.d[:, b], T.xp[:, b], T.le[:, b], Alu.subtract).then_inc(sem["d" + k], 1)
 
-    for i, (a, z) in enumerate(HALF):
-        for b in blocks(i):
-            SY.wait_ge(sem["y%d" % b], 1)
-        SY.dma_start(T.y[:, a:z], T.yb[:, a:z]).then_inc(sem["st%d" % i], 16)
-    for i in range(len(HALF)):
+    def v_m(k):
+        b = sl(BL[k])
+        V.tensor_tensor(T.mx[:, b], T.xp[:, b], T.le[:, b], Alu.max).then_inc(sem["m" + k], 1)
+
+    def v_A(k):
+        b = sl(BL[k])
+        V.wait_ge(sem["m" + k], 1)
+        V.wait_ge(sem["q" + k], 1)
+        V.tensor_tensor(T.mx[:, b], T.mx[:, b], T.q[:, b], Alu.add).then_inc(sem["A" + k], 1)
+
+    V.wait_ge(sem.xpc, 2)
+    V.wait_ge(sem.aeT, n_p)
+    v_d("O0")
+    v_m("O0")
+    V.wait_ge(sem.aeR, n_p)
+    v_d("O1")
+    v_m("O1")
+    v_A("O0")
+    v_A("O1")
+    V.wait_ge(sem.alO, n_n)
+    V.wait_ge(sem.AO0, 1)
+    V.wait_ge(sem.AO1, 1)
+    V.tensor_tensor(T.t[:, O], T.mx[:, O], T.ll[:, O], Alu.subtract).then_inc(sem.tO, 1)
+    V.wait_ge(sem.aeG, n_p)
+    v_d("G0")
+    v_d("G1")
+    V.wait_ge(sem.uO, 2)
+    V.wait_ge(sem.sO, 1)
+    V.tensor_tensor(T.yp[:, :], T.uo[:, 128:128 + W], T.sg[:, O], Alu.mult).then_inc(sem.ybk, 1)
+    V.tensor_tensor(T.yb[:, O], T.uo[:, 0:W], T.sg[:, O], Alu.mult).then_inc(sem.ya, 1)
+    v_m("G0")
+    v_m("G1")
+    v_A("G0")
+    v_A("G1")
+    V.wait_ge(sem.alG, n_n)
+    for k in ("G0", "G1"):
+        b = sl(BL[k])
+        V.wait_ge(sem["A" + k], 1)
+        V.tensor_tensor(T.t[:, b], T.mx[:, b], T.ll[:, b], Alu.subtract).then_inc(sem["t" + k], 1)
+    V.wait_ge(sem.uG0, 1)
+    V.wait_ge(sem.uG1, 1)
+    for k in ("G0", "G1"):
+        b = sl(BL[k])
+        V.wait_ge(sem["s" + k], 1)
+        V.tensor_tensor(T.yb[:, b], T.ug[:, b], T.sg[:, b], Alu.mult).then_inc(sem["y" + k], 1)
+
+    SY.wait_ge(sem.ya, 1)
+    SY.dma_start(T.y[:, O], T.yb[:, O]).then_inc(sem.st0, 16)
+    SY.wait_ge(sem.yfp, n_p)
+    SY.dma_start(T.y[:, sl(op)], T.yb[:, sl(op)]).then_inc(sem.st1, 16)
+    SY.wait_ge(sem.yfn, n_n)
+    SY.dma_start(T.y[:, sl(on)], T.yb[:, sl(on)]).then_inc(sem.st2, 16)
+    for i in range(5):
         SY.wait_ge(sem["st%d" % i], 16)
     g.wait_ge(sem.sent, sent)

@@ -5,15 +5,21 @@ W = 96
 W0 = 32
 G0 = 3 * W
 GB = [(G0, G0 + 112), (G0 + 112, C)]
-S_, B0, P_, Q_, C0 = 0.9856620329846286, -0.5526687774740315, 0.8233585316291777, 0.9998044627794158, -0.9989902994791405
+TAU, A1, K1, B1, CQ = 4.852544712059991, 4.847225890718688, 0.030821569856468722, 0.10596288389530328, -0.0035931603833465795
+ZA, ZB, ZC = -0.9778150126686176, 0.9463240450083561, -0.20580595372680266
 
 SCRATCH = {
     "xs": ("sbuf", [128, C], "float32"),
     "le": ("sbuf", [128, C], "float32"),
     "ll": ("sbuf", [128, C], "float32"),
     "d": ("sbuf", [128, C], "float32"),
-    "ad": ("sbuf", [128, C], "float32"),
-    "w": ("sbuf", [128, C], "float32"),
+    "mn": ("sbuf", [128, W], "float32"),
+    "nd": ("sbuf", [128, W], "float32"),
+    "x1": ("sbuf", [128, W], "float32"),
+    "s1": ("sbuf", [128, W], "float32"),
+    "x2": ("sbuf", [128, W], "float32"),
+    "s2": ("sbuf", [128, W], "float32"),
+    "z": ("sbuf", [128, C], "float32"),
     "q": ("sbuf", [128, C], "float32"),
     "t": ("sbuf", [128, C], "float32"),
     "sg": ("sbuf", [128, C], "float32"),
@@ -23,15 +29,15 @@ SCRATCH = {
     "xp": ("psum", [128, 512], "float32"),
     "mx": ("psum", [128, 512], "float32"),
     "uo": ("psum", [128, 512], "float32"),
+    "un": ("psum", [128, 512], "float32"),
     "ug": ("psum", [128, 512], "float32"),
 }
 
-SEMAPHORES = ["sent", "aeT", "aeR", "alO", "aeG", "alG", "yfp", "yfn", "xpc", "uO", "tO", "yc", "sO", "ybk", "ya"]
+SEMAPHORES = ["sent", "aeT", "aeR", "alO", "aeG", "alG", "yfp", "yfn", "xpc", "uO", "unO", "tO", "yc", "sO", "ybk", "ya"]
+SEMAPHORES += ["dO0", "dO1", "mO", "nO", "ndO", "x1O", "s1O", "x2O", "s2O", "AO"]
 SEMAPHORES += ["ld%d" % _i for _i in range(5)] + ["st%d" % _i for _i in range(5)]
-for _k in ("O0", "O1", "G0", "G1"):
-    SEMAPHORES += [n + _k for n in ("d", "m", "ab", "w", "q", "A")]
 for _k in ("G0", "G1"):
-    SEMAPHORES += [n + _k for n in ("u", "t", "s", "y")]
+    SEMAPHORES += [n + _k for n in ("d", "m", "u", "z", "q", "A", "t", "s", "y")]
 
 
 def engines(mask):
@@ -60,8 +66,9 @@ def rank_program(g, core, T, topo):
         return (W * r, W * r + W)
 
     own = owned(rank)
-    BL = {"O0": (own[0], own[0] + W0), "O1": (own[0] + W0, own[1]), "G0": GB[0], "G1": GB[1]}
+    BL = {"G0": GB[0], "G1": GB[1]}
     O, G = sl(own), slice(G0, C)
+    O0, O1 = slice(own[0], own[0] + W0), slice(own[0] + W0, own[1])
     on, op = owned(rn), owned(rp)
     first, rest = (on[0], on[0] + W0), (on[0] + W0, on[1])
 
@@ -88,35 +95,30 @@ def rank_program(g, core, T, topo):
     n_p = engines(topo.mask(prv, core))
     n_n = engines(topo.mask(nxt, core))
 
-    def s_lse(k):
-        b = sl(BL[k])
-        S.wait_ge(sem["d" + k], 1)
-        S.activation(T.ad[:, b], T.d[:, b], Act.Abs).then_inc(sem["ab" + k], 1)
-        S.wait_ge(sem["ab" + k], 1)
-        S.activation(T.w[:, b], T.ad[:, b], Act.Sigmoid, bias=B0, scale=-S_).then_inc(sem["w" + k], 1)
-        S.wait_ge(sem["w" + k], 1)
-        S.activation(T.q[:, b], T.w[:, b], Act.Square, bias=Q_, scale=P_).then_inc(sem["q" + k], 1)
-
     S.wait_ge(sem.ld3, 16)
     S.activation(T.xp[:, O], T.xs[:, O], Act.Copy).then_inc(sem.xpc, 1)
     S.wait_ge(sem.ld4, 16)
     S.activation(T.xp[:, G], T.xs[:, G], Act.Copy).then_inc(sem.xpc, 1)
-    s_lse("O0")
-    s_lse("O1")
-    S.activation(T.uo[:, 0:W], T.d[:, O], Act.Sigmoid).then_inc(sem.uO, 1)
-    S.activation(T.uo[:, 128:128 + W], T.d[:, O], Act.Sigmoid, bias=0.0, scale=-1.0).then_inc(sem.uO, 1)
+    S.wait_ge(sem.dO0, 1)
+    S.activation(T.uo[:, 0:W0], T.d[:, O0], Act.Sigmoid).then_inc(sem.uO, 1)
+    S.wait_ge(sem.dO1, 1)
+    S.activation(T.un[:, 0:W], T.d[:, O], Act.Sigmoid, bias=0.0, scale=-1.0).then_inc(sem.unO, 1)
     S.wait_ge(sem.tO, 1)
-    S.activation(T.yn[:, :], T.t[:, O], Act.Sigmoid, bias=-C0, scale=-1.0).then_inc(sem.yc, 1)
-    S.activation(T.sg[:, O], T.t[:, O], Act.Sigmoid, bias=C0, scale=1.0).then_inc(sem.sO, 1)
-    for k in ("G0", "G1"):
-        s_lse(k)
+    S.activation(T.yn[:, :], T.t[:, O], Act.Sigmoid, bias=-CQ, scale=-1.0).then_inc(sem.yc, 1)
+    S.activation(T.sg[:, O], T.t[:, O], Act.Sigmoid, bias=CQ, scale=1.0).then_inc(sem.sO, 1)
+    S.activation(T.uo[:, W0:W], T.d[:, O1], Act.Sigmoid).then_inc(sem.uO, 1)
     for k in ("G0", "G1"):
         b = sl(BL[k])
+        S.wait_ge(sem["d" + k], 1)
         S.activation(T.ug[:, b], T.d[:, b], Act.Sigmoid).then_inc(sem["u" + k], 1)
+        S.wait_ge(sem["u" + k], 1)
+        S.activation(T.z[:, b], T.ug[:, b], Act.Abs, bias=-0.5, scale=1.0).then_inc(sem["z" + k], 1)
+        S.wait_ge(sem["z" + k], 1)
+        S.activation(T.q[:, b], T.z[:, b], Act.Square, bias=ZB, scale=ZA).then_inc(sem["q" + k], 1)
     for k in ("G0", "G1"):
         b = sl(BL[k])
         S.wait_ge(sem["t" + k], 1)
-        S.activation(T.sg[:, b], T.t[:, b], Act.Sigmoid, bias=C0, scale=1.0).then_inc(sem["s" + k], 1)
+        S.activation(T.sg[:, b], T.t[:, b], Act.Sigmoid, bias=ZC, scale=1.0).then_inc(sem["s" + k], 1)
     for i, k in ((3, "G0"), (4, "G1")):
         b = sl(BL[k])
         S.wait_ge(sem["y" + k], 1)
@@ -138,26 +140,37 @@ def rank_program(g, core, T, topo):
 
     V.wait_ge(sem.xpc, 2)
     V.wait_ge(sem.aeT, n_p)
-    v_d("O0")
-    v_m("O0")
+    V.tensor_tensor(T.d[:, O0], T.xp[:, O0], T.le[:, O0], Alu.subtract).then_inc(sem.dO0, 1)
     V.wait_ge(sem.aeR, n_p)
-    v_d("O1")
-    v_m("O1")
-    v_A("O0")
-    v_A("O1")
+    V.tensor_tensor(T.d[:, O1], T.xp[:, O1], T.le[:, O1], Alu.subtract).then_inc(sem.dO1, 1)
+    V.tensor_tensor(T.mx[:, O], T.xp[:, O], T.le[:, O], Alu.max).then_inc(sem.mO, 1)
+    V.tensor_tensor(T.mn[:, :], T.xp[:, O], T.le[:, O], Alu.min).then_inc(sem.nO, 1)
+    V.wait_ge(sem.mO, 1)
+    V.wait_ge(sem.nO, 1)
+    V.tensor_tensor(T.nd[:, :], T.mn[:, :], T.mx[:, O], Alu.subtract).then_inc(sem.ndO, 1)
+    V.wait_ge(sem.ndO, 1)
+    V.tensor_scalar(T.x1[:, :], T.nd[:, :], -TAU, A1, Alu.max, Alu.add).then_inc(sem.x1O, 1)
+    V.wait_ge(sem.x1O, 1)
+    V.tensor_tensor(T.s1[:, :], T.x1[:, :], T.x1[:, :], Alu.mult).then_inc(sem.s1O, 1)
+    V.wait_ge(sem.s1O, 1)
+    V.tensor_scalar(T.x2[:, :], T.s1[:, :], K1, B1, Alu.mult, Alu.add).then_inc(sem.x2O, 1)
+    V.wait_ge(sem.x2O, 1)
+    V.tensor_tensor(T.s2[:, :], T.x2[:, :], T.x2[:, :], Alu.mult).then_inc(sem.s2O, 1)
+    V.wait_ge(sem.s2O, 1)
+    V.tensor_tensor(T.mx[:, O], T.mx[:, O], T.s2[:, :], Alu.add).then_inc(sem.AO, 1)
     V.wait_ge(sem.alO, n_n)
-    V.wait_ge(sem.AO0, 1)
-    V.wait_ge(sem.AO1, 1)
+    V.wait_ge(sem.AO, 1)
     V.tensor_tensor(T.t[:, O], T.mx[:, O], T.ll[:, O], Alu.subtract).then_inc(sem.tO, 1)
     V.wait_ge(sem.aeG, n_p)
     v_d("G0")
     v_d("G1")
-    V.wait_ge(sem.uO, 2)
+    V.wait_ge(sem.unO, 1)
     V.wait_ge(sem.sO, 1)
-    V.tensor_tensor(T.yp[:, :], T.uo[:, 128:128 + W], T.sg[:, O], Alu.mult).then_inc(sem.ybk, 1)
-    V.tensor_tensor(T.yb[:, O], T.uo[:, 0:W], T.sg[:, O], Alu.mult).then_inc(sem.ya, 1)
+    V.tensor_tensor(T.yp[:, :], T.un[:, 0:W], T.sg[:, O], Alu.mult).then_inc(sem.ybk, 1)
     v_m("G0")
     v_m("G1")
+    V.wait_ge(sem.uO, 2)
+    V.tensor_tensor(T.yb[:, O], T.uo[:, 0:W], T.sg[:, O], Alu.mult).then_inc(sem.ya, 1)
     v_A("G0")
     v_A("G1")
     V.wait_ge(sem.alG, n_n)
@@ -165,8 +178,8 @@ def rank_program(g, core, T, topo):
         b = sl(BL[k])
         V.wait_ge(sem["A" + k], 1)
         V.tensor_tensor(T.t[:, b], T.mx[:, b], T.ll[:, b], Alu.subtract).then_inc(sem["t" + k], 1)
-    V.wait_ge(sem.uG0, 1)
-    V.wait_ge(sem.uG1, 1)
+    V.wait_ge(sem.zG0, 1)
+    V.wait_ge(sem.zG1, 1)
     for k in ("G0", "G1"):
         b = sl(BL[k])
         V.wait_ge(sem["s" + k], 1)

from concourse.mybir import AluOpType, ActivationFunctionType

C = 512
W = 96
W0 = 32
G0 = 3 * W
GB = [(G0, G0 + 112), (G0 + 112, C)]
TAU, A1, K1, B1, CQ = 4.852544712059991, 4.847225890718688, 0.030821569856468722, 0.10596288389530328, -0.0035931603833465795
ZA, ZB, ZC = -0.9778150126686176, 0.9463240450083561, -0.20580595372680266

SCRATCH = {
    "xs": ("sbuf", [128, C], "float32"),
    "le": ("sbuf", [128, C], "float32"),
    "ll": ("sbuf", [128, C], "float32"),
    "d": ("sbuf", [128, C], "float32"),
    "mn": ("sbuf", [128, W], "float32"),
    "nd": ("sbuf", [128, W], "float32"),
    "x1": ("sbuf", [128, W], "float32"),
    "s1": ("sbuf", [128, W], "float32"),
    "x2": ("sbuf", [128, W], "float32"),
    "s2": ("sbuf", [128, W], "float32"),
    "z": ("sbuf", [128, C], "float32"),
    "q": ("sbuf", [128, C], "float32"),
    "t": ("sbuf", [128, C], "float32"),
    "sg": ("sbuf", [128, C], "float32"),
    "yb": ("sbuf", [128, C], "bfloat16"),
    "yn": ("sbuf", [128, W], "bfloat16"),
    "yp": ("sbuf", [128, W], "bfloat16"),
    "xp": ("psum", [128, 512], "float32"),
    "mx": ("psum", [128, 512], "float32"),
    "uo": ("psum", [128, 512], "float32"),
    "un": ("psum", [128, 512], "float32"),
    "ug": ("psum", [128, 512], "float32"),
}

SEMAPHORES = ["sent", "aeT", "aeR", "alO", "aeG", "alG", "yfp", "yfn", "xpc", "uO", "unO", "tO", "yc", "sO", "ybk", "ya"]
SEMAPHORES += ["dO0", "dO1", "mO", "nO", "ndO", "x1O", "s1O", "x2O", "s2O", "AO"]
SEMAPHORES += ["ld%d" % _i for _i in range(5)] + ["st%d" % _i for _i in range(5)]
for _k in ("G0", "G1"):
    SEMAPHORES += [n + _k for n in ("d", "m", "u", "z", "q", "A", "t", "s", "y")]


def engines(mask):
    return bin(mask).count("1")


def rank_program(g, core, T, topo):
    rank = T.rank_of(core)
    if rank is None:
        return
    n = len(T.cores)
    rn, rp = (rank + 1) % n, (rank - 1) % n
    nxt, prv = T.cores[rn], T.cores[rp]
    for dst in (nxt, prv):
        if not topo.may_write(core, dst):
            raise ValueError("core %d owns no port towards core %d" % (core, dst))
    sem = T.sem
    V, S, SY = g.vector, g.scalar, g.sync
    Act = ActivationFunctionType
    Alu = AluOpType

    def sl(p):
        return slice(p[0], p[1])

    def owned(r):
        return (W * r, W * r + W)

    own = owned(rank)
    BL = {"G0": GB[0], "G1": GB[1]}
    O, G = sl(own), slice(G0, C)
    O0, O1 = slice(own[0], own[0] + W0), slice(own[0] + W0, own[1])
    on, op = owned(rn), owned(rp)
    first, rest = (on[0], on[0] + W0), (on[0] + W0, on[1])

    for i, p in enumerate((first, rest, op, own, (G0, C))):
        SY.dma_start(T.xs[:, sl(p)], T.x[:, sl(p)]).then_inc(sem["ld%d" % i], 16)

    rid_n, pid_n, _ = topo.addr(nxt)
    rid_p, pid_p, _ = topo.addr(prv)
    m_n, m_p = topo.mask(core, nxt), topo.mask(core, prv)
    g.wait_ge(sem.ld0, 16)
    g.remote_dma(T.le[:, sl(first)], T.xs[:, sl(first)], sem.aeT, sem.sent, pid_n, rid_n, m_n)
    g.wait_ge(sem.ld1, 16)
    g.remote_dma(T.le[:, sl(rest)], T.xs[:, sl(rest)], sem.aeR, sem.sent, pid_n, rid_n, m_n)
    g.wait_ge(sem.ld2, 16)
    g.remote_dma(T.ll[:, sl(op)], T.xs[:, sl(op)], sem.alO, sem.sent, pid_p, rid_p, m_p)
    g.wait_ge(sem.ld4, 16)
    g.remote_dma(T.le[:, G], T.xs[:, G], sem.aeG, sem.sent, pid_n, rid_n, m_n)
    g.remote_dma(T.ll[:, G], T.xs[:, G], sem.alG, sem.sent, pid_p, rid_p, m_p)
    g.wait_ge(sem.yc, 1)
    g.remote_dma(T.yb[:, O], T.yn[:, :], sem.yfp, sem.sent, pid_n, rid_n, m_n)
    g.wait_ge(sem.ybk, 1)
    g.remote_dma(T.yb[:, O], T.yp[:, :], sem.yfn, sem.sent, pid_p, rid_p, m_p)
    sent = 4 * engines(m_n) + 3 * engines(m_p)
    n_p = engines(topo.mask(prv, core))
    n_n = engines(topo.mask(nxt, core))

    S.wait_ge(sem.ld3, 16)
    S.activation(T.xp[:, O], T.xs[:, O], Act.Copy).then_inc(sem.xpc, 1)
    S.wait_ge(sem.ld4, 16)
    S.activation(T.xp[:, G], T.xs[:, G], Act.Copy).then_inc(sem.xpc, 1)
    S.wait_ge(sem.dO0, 1)
    S.activation(T.uo[:, 0:W0], T.d[:, O0], Act.Sigmoid).then_inc(sem.uO, 1)
    S.wait_ge(sem.dO1, 1)
    S.activation(T.un[:, 0:W], T.d[:, O], Act.Sigmoid, bias=0.0, scale=-1.0).then_inc(sem.unO, 1)
    S.wait_ge(sem.tO, 1)
    S.activation(T.yn[:, :], T.t[:, O], Act.Sigmoid, bias=-CQ, scale=-1.0).then_inc(sem.yc, 1)
    S.activation(T.sg[:, O], T.t[:, O], Act.Sigmoid, bias=CQ, scale=1.0).then_inc(sem.sO, 1)
    S.activation(T.uo[:, W0:W], T.d[:, O1], Act.Sigmoid).then_inc(sem.uO, 1)
    for k in ("G0", "G1"):
        b = sl(BL[k])
        S.wait_ge(sem["d" + k], 1)
        S.activation(T.ug[:, b], T.d[:, b], Act.Sigmoid).then_inc(sem["u" + k], 1)
        S.wait_ge(sem["u" + k], 1)
        S.activation(T.z[:, b], T.ug[:, b], Act.Abs, bias=-0.5, scale=1.0).then_inc(sem["z" + k], 1)
        S.wait_ge(sem["z" + k], 1)
        S.activation(T.q[:, b], T.z[:, b], Act.Square, bias=ZB, scale=ZA).then_inc(sem["q" + k], 1)
    for k in ("G0", "G1"):
        b = sl(BL[k])
        S.wait_ge(sem["t" + k], 1)
        S.activation(T.sg[:, b], T.t[:, b], Act.Sigmoid, bias=ZC, scale=1.0).then_inc(sem["s" + k], 1)
    for i, k in ((3, "G0"), (4, "G1")):
        b = sl(BL[k])
        S.wait_ge(sem["y" + k], 1)
        S.dma_start(T.y[:, b], T.yb[:, b]).then_inc(sem["st%d" % i], 16)

    def v_d(k):
        b = sl(BL[k])
        V.tensor_tensor(T.d[:, b], T.xp[:, b], T.le[:, b], Alu.subtract).then_inc(sem["d" + k], 1)

    def v_m(k):
        b = sl(BL[k])
        V.tensor_tensor(T.mx[:, b], T.xp[:, b], T.le[:, b], Alu.max).then_inc(sem["m" + k], 1)

    def v_A(k):
        b = sl(BL[k])
        V.wait_ge(sem["m" + k], 1)
        V.wait_ge(sem["q" + k], 1)
        V.tensor_tensor(T.mx[:, b], T.mx[:, b], T.q[:, b], Alu.add).then_inc(sem["A" + k], 1)

    V.wait_ge(sem.xpc, 2)
    V.wait_ge(sem.aeT, n_p)
    V.tensor_tensor(T.d[:, O0], T.xp[:, O0], T.le[:, O0], Alu.subtract).then_inc(sem.dO0, 1)
    V.wait_ge(sem.aeR, n_p)
    V.tensor_tensor(T.d[:, O1], T.xp[:, O1], T.le[:, O1], Alu.subtract).then_inc(sem.dO1, 1)
    V.tensor_tensor(T.mx[:, O], T.xp[:, O], T.le[:, O], Alu.max).then_inc(sem.mO, 1)
    V.tensor_tensor(T.mn[:, :], T.xp[:, O], T.le[:, O], Alu.min).then_inc(sem.nO, 1)
    V.wait_ge(sem.mO, 1)
    V.wait_ge(sem.nO, 1)
    V.tensor_tensor(T.nd[:, :], T.mn[:, :], T.mx[:, O], Alu.subtract).then_inc(sem.ndO, 1)
    V.wait_ge(sem.ndO, 1)
    V.tensor_scalar(T.x1[:, :], T.nd[:, :], -TAU, A1, Alu.max, Alu.add).then_inc(sem.x1O, 1)
    V.wait_ge(sem.x1O, 1)
    V.tensor_tensor(T.s1[:, :], T.x1[:, :], T.x1[:, :], Alu.mult).then_inc(sem.s1O, 1)
    V.wait_ge(sem.s1O, 1)
    V.tensor_scalar(T.x2[:, :], T.s1[:, :], K1, B1, Alu.mult, Alu.add).then_inc(sem.x2O, 1)
    V.wait_ge(sem.x2O, 1)
    V.tensor_tensor(T.s2[:, :], T.x2[:, :], T.x2[:, :], Alu.mult).then_inc(sem.s2O, 1)
    V.wait_ge(sem.s2O, 1)
    V.tensor_tensor(T.mx[:, O], T.mx[:, O], T.s2[:, :], Alu.add).then_inc(sem.AO, 1)
    V.wait_ge(sem.alO, n_n)
    V.wait_ge(sem.AO, 1)
    V.tensor_tensor(T.t[:, O], T.mx[:, O], T.ll[:, O], Alu.subtract).then_inc(sem.tO, 1)
    V.wait_ge(sem.aeG, n_p)
    v_d("G0")
    v_d("G1")
    V.wait_ge(sem.unO, 1)
    V.wait_ge(sem.sO, 1)
    V.tensor_tensor(T.yp[:, :], T.un[:, 0:W], T.sg[:, O], Alu.mult).then_inc(sem.ybk, 1)
    v_m("G0")
    v_m("G1")
    V.wait_ge(sem.uO, 2)
    V.tensor_tensor(T.yb[:, O], T.uo[:, 0:W], T.sg[:, O], Alu.mult).then_inc(sem.ya, 1)
    v_A("G0")
    v_A("G1")
    V.wait_ge(sem.alG, n_n)
    for k in ("G0", "G1"):
        b = sl(BL[k])
        V.wait_ge(sem["A" + k], 1)
        V.tensor_tensor(T.t[:, b], T.mx[:, b], T.ll[:, b], Alu.subtract).then_inc(sem["t" + k], 1)
    V.wait_ge(sem.zG0, 1)
    V.wait_ge(sem.zG1, 1)
    for k in ("G0", "G1"):
        b = sl(BL[k])
        V.wait_ge(sem["s" + k], 1)
        V.tensor_tensor(T.yb[:, b], T.ug[:, b], T.sg[:, b], Alu.mult).then_inc(sem["y" + k], 1)

    SY.wait_ge(sem.ya, 1)
    SY.dma_start(T.y[:, O], T.yb[:, O]).then_inc(sem.st0, 16)
    SY.wait_ge(sem.yfp, n_p)
    SY.dma_start(T.y[:, sl(op)], T.yb[:, sl(op)]).then_inc(sem.st1, 16)
    SY.wait_ge(sem.yfn, n_n)
    SY.dma_start(T.y[:, sl(on)], T.yb[:, sl(on)]).then_inc(sem.st2, 16)
    for i in range(5):
        SY.wait_ge(sem["st%d" % i], 16)
    g.wait_ge(sem.sent, sent)
